import numpy as np
import ml_dtypes


def mxq(x, axis, fmt="e4m3"):
    dtype, down = {"e4m3": (ml_dtypes.float8_e4m3fn, 7), "e5m2": (ml_dtypes.float8_e5m2, 14)}[fmt]
    v = np.moveaxis(np.asarray(x, np.float32).astype(ml_dtypes.bfloat16).astype(np.float64), axis, -1)
    blocks = v.reshape(v.shape[:-1] + (-1, 32))
    amax = np.abs(blocks).max(-1, keepdims=True)
    byte = np.maximum(np.where(amax > 0, np.frexp(amax)[1] - 1 + 127, 0) - down, 1)
    scale = np.exp2(byte - 127.0)
    codes = (blocks / scale).astype(np.float32).astype(dtype).astype(np.float64)
    return np.moveaxis((codes * scale).reshape(v.shape), -1, axis)


WIDE = False


def mx_kscale(k):
    if not WIDE:
        return np.ones(k)
    levels = np.array([10, -10, 5, -5, 0])
    if k % 512:
        return np.exp2(np.random.permutation(np.resize(levels, k // 32))).repeat(32)
    a = np.empty((k // 512, 16))
    for p in range(k // 512):
        a[p, :8] = np.random.permutation(np.resize(levels, 8))
        for g in range(8):
            far = levels[np.abs(levels - a[p, g]) >= 10]
            a[p, g + 8] = far[np.random.randint(len(far))]
    return np.exp2(a.ravel()).repeat(32)


def f64(x):
    return np.asarray(x).astype(np.float64)


def striped(idx):
    return np.tile(idx.reshape(-1, 16).T, (8, 1)).astype(np.uint16)


def unstriped(offs):
    return offs[:16].T.reshape(-1).astype(np.int64)


def pack_weight(w):
    k, n = w.shape
    w = f64(np.asarray(w, np.float32).astype(ml_dtypes.bfloat16)).reshape(k // 32, 32, n)
    amax = np.abs(w).max(1)
    byte = np.clip(np.where(amax > 0, np.frexp(amax)[1] - 1 + 127 - 7, 1), 1, 254)
    scaled = (w * np.exp2(127.0 - byte)[:, None, :]).reshape(k, n).astype(np.float32)
    words = np.ascontiguousarray(scaled.reshape(k // 512, 128, 4, n).transpose(0, 1, 3, 2)).astype(ml_dtypes.float8_e4m3fn).view(np.uint8)
    return words, np.ascontiguousarray(byte.astype(np.uint8).reshape(k // 512, 16, n))


def unpack_weight(words, scales):
    g, p, n, _ = words.shape
    vals = np.ascontiguousarray(words).view(ml_dtypes.float8_e4m3fn).astype(np.float64) * np.repeat(np.exp2(scales.astype(np.float64) - 127.0), 8, axis=1)[..., None]
    return vals.transpose(0, 1, 3, 2).reshape(g * 512, n)


K, T, S, N, H = 1024, 1024, 512, 256, 512


def setup_inputs():
    n = np.random.standard_normal
    s = mx_kscale(K)[:, None]
    u = mx_kscale(H)
    packed_xT = pack_weight(n((K, T)) * s)
    return {
        "x_words": packed_xT[0],
        "x_scales": packed_xT[1],
        "w1": (n((K, H)) / np.sqrt(K) / s).astype(np.float32),
        "w2": (n((K, H)) / np.sqrt(K) / s).astype(np.float32),
        "u1": (n((H, S))).astype(np.float32),
        "u2": (n((H, S))).astype(np.float32),
        "thr": (np.random.uniform(0.3, 1.0, (H, S))).astype(np.float32),
        "unit": (np.random.uniform(0.6, 1.4, (H, 1)) * u[:, None]).astype(np.float32),
        "w3": (n((H, N)) / np.sqrt(H) / u[:, None]).astype(np.float32),
        "offs": striped(np.random.permutation(T)[:S]),
        "mod": striped(np.random.permutation(S)),
    }


def reference(x_words, x_scales, w1, w2, u1, u2, thr, unit, w3, offs, mod):
    xq = unpack_weight(x_words, x_scales)[:, unstriped(offs)]
    la = mxq(f64(w1), 0, "e4m3").T @ xq
    lb = mxq(f64(w2), 0, "e4m3").T @ xq
    alg = la * f64(u1) + lb * f64(u2)
    lm = la[:, unstriped(mod)]
    grad = (la) ** 2 + (lb) ** 2 + 0.5 * ((lm) ** 2) + 0.3
    samp = ((alg) ** 2) / grad
    gm = f64(thr) / (samp + f64(thr))
    hid = f64(unit) * (gm * alg)
    return mxq(f64(w3), 0, "e4m3").T @ mxq(hid, 0, "e4m3")

@@ -1,0 +1,306 @@
+from contextlib import ExitStack
+
+import concourse.mybir as mybir
+
+K, T, S, N, H = 1024, 1024, 512, 256, 512
+FLOPS = 2 * (2 * K * H * S + H * N * S)
+
+F32 = mybir.dt.float32
+BF16 = mybir.dt.bfloat16
+I32 = mybir.dt.int32
+U32 = mybir.dt.uint32
+U16 = mybir.dt.uint16
+U8 = mybir.dt.uint8
+FP8X4 = mybir.dt.float8_e4m3fn_x4
+ALU = mybir.AluOpType
+ACT = mybir.ActivationFunctionType
+
+P = 128
+PACK = 4
+K_PASS = P * PACK
+PASSES = K // K_PASS
+CHUNK = 128
+CHUNKS = S // CHUNK
+HALF = S // 2
+
+
+def tile_picked_ysampso_wres_p_kernel(
+    tc, x_words, x_scales, w1, w2, u1, u2, thr, unit, w3, offs, mod, out
+):
+    nc = tc.nc
+    with ExitStack() as ctx:
+        lists = ctx.enter_context(tc.tile_pool(name="lists", bufs=1))
+        keep = ctx.enter_context(tc.tile_pool(name="keep", bufs=1))
+        work = ctx.enter_context(tc.tile_pool(name="work", bufs=3))
+        psum = ctx.enter_context(tc.psum_pool(name="psum", bufs=1))
+
+        offs_sb = lists.tile([P, S // 16], U16, name="offs_sb")
+        mod_sb = lists.tile([P, S // 16], U16, name="mod_sb")
+
+        table_scales = keep.tile([P, T], U8, name="table_scales", align_bytes=64)
+        landed_scales = keep.tile([P, T], U8, name="landed_scales", align_bytes=64)
+        nc.vector.memset(table_scales[:].bitcast(I32), 0)
+        for quad in range(4):
+            rows = slice(32 * quad, 32 * quad + 4 * PASSES)
+            nc.sync.dma_start(
+                landed_scales[rows, :].bitcast(I32), x_scales[:, 4 * quad : 4 * quad + 4, :].bitcast(I32)
+            )
+        for quad in range(4):
+            rows = slice(32 * quad, 32 * quad + 4 * PASSES)
+            nc.vector.tensor_copy(table_scales[rows, :].bitcast(I32), landed_scales[rows, :].bitcast(I32))
+        unit_sb = keep.tile([P, PACK], F32, name="unit_sb")
+        nc.sync.dma_start(unit_sb[:], unit.rearrange("(p t) o -> p (t o)", t=PACK))
+        nc.sync.dma_start(offs_sb[:], offs)
+
+        table_words = [keep.tile([P, T], U32, name="table_words%d" % o, align_bytes=64) for o in range(PASSES)]
+        w_raw = [
+            [keep.tile([P, PACK, H], F32, name="w_raw%d_%d" % (a, o), tag="w_raw%d_%d" % (a, o)) for o in range(PASSES)] for a in range(2)
+        ]
+
+        def load_table(o):
+            nc.sync.dma_start(
+                table_words[o][:].bitcast(I32), x_words[o].rearrange("p n t -> p (n t)").bitcast(I32)
+            )
+
+        def load_weight(a, w, o):
+            rows = w[o * K_PASS : (o + 1) * K_PASS, :]
+            nc.sync.dma_start(w_raw[a][o][:], rows.rearrange("(p j) c -> p j c", j=PACK))
+
+        load_table(0)
+        load_weight(0, w1, 0)
+        load_table(1)
+        load_weight(0, w1, 1)
+        nc.sync.dma_start(mod_sb[:], mod)
+        u1_sb = keep.tile([P, PACK, S], F32, name="u1_sb")
+        nc.sync.dma_start(u1_sb[:], u1.rearrange("(p t) j -> p t j", t=PACK))
+        load_weight(1, w2, 0)
+        load_weight(1, w2, 1)
+        u2_sb = [keep.tile([P, PACK, HALF], F32, name="u2_sb%d" % h) for h in range(2)]
+        thr_sb = [keep.tile([P, PACK, HALF], F32, name="thr_sb%d" % h) for h in range(2)]
+        for h in range(2):
+            cols = slice(h * HALF, (h + 1) * HALF)
+            nc.sync.dma_start(u2_sb[h][:], u2[:, cols].rearrange("(p t) j -> p t j", t=PACK))
+            nc.sync.dma_start(thr_sb[h][:], thr[:, cols].rearrange("(p t) j -> p t j", t=PACK))
+        w3_raw = keep.tile([P, PACK, N], F32, name="w3_raw")
+        nc.sync.dma_start(w3_raw[:], w3.rearrange("(p j) c -> p j c", j=PACK))
+
+        unit_safe = keep.tile([P, PACK], F32, name="unit_safe")
+        unit_root = keep.tile([P, PACK], F32, name="unit_root")
+        unit_guess = keep.tile([P, PACK], F32, name="unit_guess")
+        unit_err = keep.tile([P, PACK], F32, name="unit_err")
+        unit_fix = keep.tile([P, PACK], F32, name="unit_fix")
+        unit_inv = keep.tile([P, PACK], F32, name="unit_inv")
+        nc.vector.scalar_tensor_tensor(unit_safe[:], unit_sb[:], 0.0, unit_sb[:], ALU.is_equal, ALU.add)
+        nc.scalar.activation(unit_root[:], unit_safe[:], ACT.Abs_reciprocal_sqrt)
+        nc.vector.tensor_tensor(unit_guess[:], unit_root[:], unit_root[:], ALU.mult)
+        nc.vector.tensor_tensor(unit_err[:], unit_guess[:], unit_safe[:], ALU.mult)
+        nc.vector.scalar_tensor_tensor(unit_fix[:], unit_err[:], -0.5, unit_err[:], ALU.mult, ALU.mult)
+        nc.vector.scalar_tensor_tensor(unit_inv[:], unit_fix[:], 1.5, unit_guess[:], ALU.add, ALU.mult)
+
+        x_codes = [keep.tile([P, S], U32, name="x_codes%d" % o, align_bytes=64) for o in range(PASSES)]
+        x_exps = keep.tile([P, S], U8, name="x_exps", align_bytes=64)
+        nc.vector.tensor_copy(x_codes[0][:], table_words[0][:].indirect(offs_sb[:]))
+        nc.vector.tensor_copy(x_exps[:], table_scales[:].indirect(offs_sb[:]))
+        nc.vector.tensor_copy(x_codes[1][:], table_words[1][:].indirect(offs_sb[:]))
+
+        w_codes = [[None] * PASSES for a in range(2)]
+        w_exps = [[None] * PASSES for a in range(2)]
+
+        def quantize_weight(a, o, casters):
+            pairs = []
+            for u in range(2):
+                grouped = keep.tile([P, 2, P, PACK], BF16, name="w_bf%d_%d_%d" % (a, o, u), align_bytes=64)
+                src = w_raw[a][o][:].rearrange("p j (m t) -> p m j t", t=PACK)[:, :, :, 2 * u : 2 * u + 2]
+                casters[u](grouped[:].rearrange("p t m j -> p m j t"), src)
+                pairs.append(grouped)
+            codes, exps = [], []
+            for u in range(2):
+                c = keep.tile([P, 2 * P], U32, name="w_codes%d_%d_%d" % (a, o, u), align_bytes=64)
+                e = keep.tile([P, 2 * P], U8, name="w_exps%d_%d_%d" % (a, o, u), align_bytes=64)
+                nc.vector.quantize_mx(
+                    out=c[:].bitcast(FP8X4), scales=e[:], in_=pairs[u][:].rearrange("p t m j -> p (t m j)")
+                )
+                codes.append(c)
+                exps.append(e)
+            w_codes[a][o] = codes
+            w_exps[a][o] = exps
+
+        def first_product(acc, a, o, t, cols, start, stop):
+            m = slice((t % 2) * P, (t % 2 + 1) * P)
+            nc.tensor.matmul_mx(
+                out=acc,
+                lhsT=w_codes[a][o][t // 2][:, m].bitcast(FP8X4),
+                lhsT_scale=w_exps[a][o][t // 2][:, m],
+                rhs=x_codes[o][:, cols].bitcast(FP8X4),
+                rhs_scale=x_exps[4 * o : P, cols],
+                start=start,
+                stop=stop,
+            )
+
+        on_scalar, on_vector = nc.scalar.copy, nc.vector.tensor_copy
+        quantize_weight(0, 0, (on_scalar, on_scalar))
+        quantize_weight(0, 1, (on_vector, on_scalar))
+
+
+        la = [psum.tile([P, S], F32, name="la%d" % t, tag="bank%d" % t) for t in range(PACK)]
+        for o in range(PASSES):
+            for t in range(PACK):
+                first_product(la[t][:], 0, o, t, slice(0, S), o == 0, o == PASSES - 1)
+
+        la_sq = [keep.tile([P, S], F32, name="la_sq%d" % t) for t in range(PACK)]
+        lm_sq = keep.tile([P, PACK, S], F32, name="lm_sq")
+        term_a = keep.tile([P, PACK, S], F32, name="term_a")
+
+        def square_la(t):
+            nc.scalar.activation(la_sq[t][:], la[t][:], ACT.Square)
+
+        def weigh_la(t):
+            nc.vector.scalar_tensor_tensor(
+                term_a[:, t, :], la[t][:], unit_sb[:, t : t + 1], u1_sb[:, t, :], ALU.mult, ALU.mult
+            )
+
+        for t in (0, 2):
+            square_la(t)
+            weigh_la(t + 1)
+        for t in (0, 2):
+            square_la(t + 1)
+            weigh_la(t)
+        for h in range(2):
+            cols = slice(h * HALF, (h + 1) * HALF)
+            for t in range(PACK):
+                nc.scalar.activation(
+                    lm_sq[:, t, cols], la_sq[t][:].indirect(mod_sb[:, 16 * h : 16 * (h + 1)]), ACT.Copy
+                )
+        quantize_weight(1, 0, (on_vector, on_vector))
+        quantize_weight(1, 1, (on_vector, on_vector))
+        grad_a = keep.tile([P, PACK, S], F32, name="grad_a", tag="w_raw1_1")
+        for h in range(2):
+            cols = slice(h * HALF, (h + 1) * HALF)
+            for t in range(PACK):
+                nc.vector.scalar_tensor_tensor(
+                    grad_a[:, t, cols], lm_sq[:, t, cols], 0.5, la_sq[t][:, cols], ALU.mult, ALU.add
+                )
+
+        lb = [psum.tile([P, PACK, CHUNK], F32, name="lb%d" % k, tag="bank%d" % (PACK + k)) for k in range(CHUNKS)]
+        for o in range(PASSES):
+            for k in range(CHUNKS):
+                for t in range(PACK):
+                    first_product(
+                        lb[k][:, t, :], 1, o, t, slice(k * CHUNK, (k + 1) * CHUNK),
+                        o == 0 and t == 0, o == PASSES - 1 and t == PACK - 1,
+                    )
+
+        w3_bf = keep.tile([P, N, PACK], BF16, name="w3_bf", align_bytes=64)
+        w3_codes = keep.tile([P, N], U32, name="w3_codes", align_bytes=64)
+        w3_exps = keep.tile([P, N], U8, name="w3_exps", align_bytes=64)
+
+        def quantize_w3():
+            nc.scalar.copy(
+                w3_bf[:].rearrange("p (c i) j -> p c j i", i=4), w3_raw[:].rearrange("p j (c i) -> p c j i", i=4)
+            )
+            nc.vector.quantize_mx(
+                out=w3_codes[:].bitcast(FP8X4), scales=w3_exps[:], in_=w3_bf[:].rearrange("p n j -> p (n j)")
+            )
+
+        pieces = [(0,128),(128,256),(256,384),(384,448),(448,512)]
+        term_b = {}
+        lb_sq = {}
+        alg = {}
+        inv_root = {}
+        gm = {}
+
+        def read_lb(k):
+            h, part = divmod(k, 2)
+            hcols = slice(part * CHUNK, (part + 1) * CHUNK)
+            lb_sq[k] = keep.tile([P, PACK, CHUNK], F32, name="lb_sq%d" % k)
+            term_b[k] = keep.tile([P, PACK, CHUNK], F32, name="term_b%d" % k)
+            if k < 2:
+                nc.vector.tensor_tensor(term_b[k][:], lb[k][:], u2_sb[h][:, :, hcols], ALU.mult)
+            nc.scalar.activation(lb_sq[k][:], lb[k][:], ACT.Square)
+            if k >= 2:
+                nc.vector.tensor_tensor(term_b[k][:], lb[k][:], u2_sb[h][:, :, hcols], ALU.mult)
+
+        def front(i):
+            lo, hi = pieces[i]
+            width = hi - lo
+            cols = slice(lo, hi)
+            k = lo // CHUNK
+            kcols = slice(lo - k * CHUNK, hi - k * CHUNK)
+            h = lo // HALF
+            hcols = slice(lo - h * HALF, hi - h * HALF)
+            grad = work.tile([P, PACK, width], F32, name="grad")
+            den = work.tile([P, PACK, width], F32, name="den")
+            alg[i] = keep.tile([P, PACK, width], F32, name="alg%d" % i)
+            inv_root[i] = work.tile([P, PACK, width], F32, name="inv_root")
+            nc.vector.tensor_tensor(grad[:], lb_sq[k][:, :, kcols], grad_a[:, :, cols], ALU.add)
+            for t in range(PACK):
+                nc.vector.scalar_tensor_tensor(
+                    alg[i][:, t, :], term_b[k][:, t, kcols], unit_sb[:, t : t + 1], term_a[:, t, cols],
+                    ALU.mult, ALU.add,
+                )
+            nc.vector.scalar_tensor_tensor(den[:], grad[:], 0.3, thr_sb[h][:, :, hcols], ALU.add, ALU.mult)
+            nc.scalar.activation(inv_root[i][:], den[:], ACT.Abs_reciprocal_sqrt)
+
+        def middle(i):
+            width = pieces[i][1] - pieces[i][0]
+            ratio = work.tile([P, PACK, width], F32, name="ratio")
+            ratio_sq = work.tile([P, PACK, width], F32, name="ratio_sq")
+            gm_root = work.tile([P, PACK, width], F32, name="gm_root")
+            gm[i] = work.tile([P, PACK, width], F32, name="gm")
+            nc.vector.tensor_tensor(ratio[:], alg[i][:], inv_root[i][:], ALU.mult)
+            for t in range(PACK):
+                nc.scalar.activation(ratio_sq[:, t, :], ratio[:, t, :], ACT.Square, scale=unit_inv[:, t : t + 1])
+            nc.scalar.activation(gm_root[:], ratio_sq[:], ACT.Abs_reciprocal_sqrt, bias=1.0)
+            nc.scalar.activation(gm[i][:], gm_root[:], ACT.Square)
+
+        def back(i):
+            lo, hi = pieces[i]
+            width = hi - lo
+            hid = work.tile([P, width, PACK], BF16, name="hid", align_bytes=64)
+            hid_codes = work.tile([P, width], U32, name="hid_codes", align_bytes=64)
+            hid_exps = work.tile([P, width], U8, name="hid_exps", align_bytes=64)
+            nc.vector.tensor_tensor(
+                hid[:].rearrange("p (c i) t -> p c t i", i=4),
+                alg[i][:].rearrange("p t (c i) -> p c t i", i=4),
+                gm[i][:].rearrange("p t (c i) -> p c t i", i=4),
+                ALU.mult,
+            )
+            nc.vector.quantize_mx(
+                out=hid_codes[:].bitcast(FP8X4), scales=hid_exps[:], in_=hid[:].rearrange("p n t -> p (n t)")
+            )
+            acc = psum.tile([P, N // P, width], F32, name="acc%d" % i, tag="bank%d" % (i % PACK))
+            for g in range(N // P):
+                m = slice(g * P, (g + 1) * P)
+                nc.tensor.matmul_mx(
+                    out=acc[:, g, :],
+                    lhsT=w3_codes[:, m].bitcast(FP8X4),
+                    lhsT_scale=w3_exps[:, m],
+                    rhs=hid_codes[:].bitcast(FP8X4),
+                    rhs_scale=hid_exps[:],
+                    start=True,
+                    stop=True,
+                )
+            result = work.tile([P, N // P, width], F32, name="result")
+            nc.scalar.copy(result[:], acc[:])
+            nc.sync.dma_start(out[:, lo:hi].rearrange("(g m) j -> m g j", m=P), result[:])
+
+        read_lb(0)
+        read_lb(1)
+        front(0)
+        middle(0)
+        read_lb(2)
+        front(1)
+        quantize_w3()
+        middle(1)
+        read_lb(3)
+        front(2)
+        middle(2)
+        front(3)
+        middle(3)
+        front(4)
+        middle(4)
+        back(0)
+        back(1)
+        back(2)
+        back(3)
+        back(4)

@@ -37,21 +37,6 @@ def tile_picked_ysampso_wres_p_kernel(
         offs_sb = lists.tile([P, S // 16], U16, name="offs_sb")
         mod_sb = lists.tile([P, S // 16], U16, name="mod_sb")
 
-        table_scales = keep.tile([P, T], U8, name="table_scales", align_bytes=64)
-        landed_scales = keep.tile([P, T], U8, name="landed_scales", align_bytes=64)
-        nc.vector.memset(table_scales[:].bitcast(I32), 0)
-        for quad in range(4):
-            rows = slice(32 * quad, 32 * quad + 4 * PASSES)
-            nc.sync.dma_start(
-                landed_scales[rows, :].bitcast(I32), x_scales[:, 4 * quad : 4 * quad + 4, :].bitcast(I32)
-            )
-        for quad in range(4):
-            rows = slice(32 * quad, 32 * quad + 4 * PASSES)
-            nc.vector.tensor_copy(table_scales[rows, :].bitcast(I32), landed_scales[rows, :].bitcast(I32))
-        unit_sb = keep.tile([P, PACK], F32, name="unit_sb")
-        nc.sync.dma_start(unit_sb[:], unit.rearrange("(p t) o -> p (t o)", t=PACK))
-        nc.sync.dma_start(offs_sb[:], offs)
-
         table_words = [keep.tile([P, T], U32, name="table_words%d" % o, align_bytes=64) for o in range(PASSES)]
         w_raw = [
             [keep.tile([P, PACK, H], F32, name="w_raw%d_%d" % (a, o), tag="w_raw%d_%d" % (a, o)) for o in range(PASSES)] for a in range(2)
@@ -66,22 +51,43 @@ def tile_picked_ysampso_wres_p_kernel(
             rows = w[o * K_PASS : (o + 1) * K_PASS, :]
             nc.sync.dma_start(w_raw[a][o][:], rows.rearrange("(p j) c -> p j c", j=PACK))
 
+        u1_sb = [keep.tile([P, PACK, HALF], F32, name="u1_sb%d" % h) for h in range(2)]
+        u2_sb = [keep.tile([P, PACK, HALF], F32, name="u2_sb%d" % h) for h in range(2)]
+        thr_sb = [keep.tile([P, PACK, HALF], F32, name="thr_sb%d" % h) for h in range(2)]
+        w3_raw = keep.tile([P, PACK, N], F32, name="w3_raw")
+
+        def load_half(tiles, src, h):
+            cols = slice(h * HALF, (h + 1) * HALF)
+            nc.sync.dma_start(tiles[h][:], src[:, cols].rearrange("(p t) j -> p t j", t=PACK))
+
         load_table(0)
+        unit_sb = keep.tile([P, PACK], F32, name="unit_sb")
+        nc.sync.dma_start(unit_sb[:], unit.rearrange("(p t) o -> p (t o)", t=PACK))
+        nc.sync.dma_start(offs_sb[:], offs)
+
+        table_scales = keep.tile([P, T], U8, name="table_scales", align_bytes=64)
+        landed_scales = keep.tile([P, T], U8, name="landed_scales", align_bytes=64)
+        nc.vector.memset(table_scales[:].bitcast(I32), 0)
+        for quad in range(4):
+            rows = slice(32 * quad, 32 * quad + 4 * PASSES)
+            nc.sync.dma_start(
+                landed_scales[rows, :].bitcast(I32), x_scales[:, 4 * quad : 4 * quad + 4, :].bitcast(I32)
+            )
+        for quad in range(4):
+            rows = slice(32 * quad, 32 * quad + 4 * PASSES)
+            nc.vector.tensor_copy(table_scales[rows, :].bitcast(I32), landed_scales[rows, :].bitcast(I32))
         load_weight(0, w1, 0)
         load_table(1)
         load_weight(0, w1, 1)
         nc.sync.dma_start(mod_sb[:], mod)
-        u1_sb = keep.tile([P, PACK, S], F32, name="u1_sb")
-        nc.sync.dma_start(u1_sb[:], u1.rearrange("(p t) j -> p t j", t=PACK))
         load_weight(1, w2, 0)
         load_weight(1, w2, 1)
-        u2_sb = [keep.tile([P, PACK, HALF], F32, name="u2_sb%d" % h) for h in range(2)]
-        thr_sb = [keep.tile([P, PACK, HALF], F32, name="thr_sb%d" % h) for h in range(2)]
-        for h in range(2):
-            cols = slice(h * HALF, (h + 1) * HALF)
-            nc.sync.dma_start(u2_sb[h][:], u2[:, cols].rearrange("(p t) j -> p t j", t=PACK))
-            nc.sync.dma_start(thr_sb[h][:], thr[:, cols].rearrange("(p t) j -> p t j", t=PACK))
-        w3_raw = keep.tile([P, PACK, N], F32, name="w3_raw")
+        load_half(u1_sb, u1, 0)
+        load_half(u2_sb, u2, 0)
+        load_half(thr_sb, thr, 0)
+        load_half(u1_sb, u1, 1)
+        load_half(u2_sb, u2, 1)
+        load_half(thr_sb, thr, 1)
         nc.sync.dma_start(w3_raw[:], w3.rearrange("(p j) c -> p j c", j=PACK))
 
         unit_safe = keep.tile([P, PACK], F32, name="unit_safe")
@@ -148,38 +154,40 @@ def tile_picked_ysampso_wres_p_kernel(
                 first_product(la[t][:], 0, o, t, slice(0, S), o == 0, o == PASSES - 1)
 
         la_sq = [keep.tile([P, S], F32, name="la_sq%d" % t) for t in range(PACK)]
-        lm_sq = keep.tile([P, PACK, S], F32, name="lm_sq")
+        lm_sq = {}
         term_a = keep.tile([P, PACK, S], F32, name="term_a")
 
-        def square_la(t):
+        for t in range(PACK):
             nc.scalar.activation(la_sq[t][:], la[t][:], ACT.Square)
 
-        def weigh_la(t):
-            nc.vector.scalar_tensor_tensor(
-                term_a[:, t, :], la[t][:], unit_sb[:, t : t + 1], u1_sb[:, t, :], ALU.mult, ALU.mult
-            )
-
-        for t in (0, 2):
-            square_la(t)
-            weigh_la(t + 1)
-        for t in (0, 2):
-            square_la(t + 1)
-            weigh_la(t)
-        for h in range(2):
-            cols = slice(h * HALF, (h + 1) * HALF)
-            for t in range(PACK):
-                nc.scalar.activation(
-                    lm_sq[:, t, cols], la_sq[t][:].indirect(mod_sb[:, 16 * h : 16 * (h + 1)]), ACT.Copy
-                )
-        quantize_weight(1, 0, (on_vector, on_vector))
-        quantize_weight(1, 1, (on_vector, on_vector))
-        grad_a = keep.tile([P, PACK, S], F32, name="grad_a", tag="w_raw1_1")
-        for h in range(2):
+        def weigh_la(h):
             cols = slice(h * HALF, (h + 1) * HALF)
             for t in range(PACK):
                 nc.vector.scalar_tensor_tensor(
-                    grad_a[:, t, cols], lm_sq[:, t, cols], 0.5, la_sq[t][:, cols], ALU.mult, ALU.add
+                    term_a[:, t, cols], la[t][:, cols], unit_sb[:, t : t + 1], u1_sb[h][:, t, :], ALU.mult, ALU.mult
                 )
+
+        def fetch_partner(h):
+            cols = slice(h * HALF, (h + 1) * HALF)
+            for t in range(PACK):
+                lm_sq[h, t] = keep.tile([P, HALF], F32, name="lm_sq%d_%d" % (h, t), tag="lm_%d" % t)
+                nc.scalar.activation(
+                    lm_sq[h, t][:], la_sq[t][:].indirect(mod_sb[:, 16 * h : 16 * (h + 1)]), ACT.Copy, scale=0.5
+                )
+
+        grad_a = {}
+
+        def add_partner(h):
+            cols = slice(h * HALF, (h + 1) * HALF)
+            grad_a[h] = keep.tile([P, PACK, HALF], F32, name="grad_a%d" % h, tag=("w_raw1_1","thr_sb0")[h])
+            for t in range(PACK):
+                adder = nc.gpsimd if True else nc.vector
+                adder.tensor_tensor(grad_a[h][:, t, :], lm_sq[h, t][:], la_sq[t][:, cols], ALU.add)
+
+        fetch_partner(0)
+        quantize_weight(1, 0, (on_vector, on_vector))
+        quantize_weight(1, 1, (on_vector, on_vector))
+        add_partner(0)
 
         lb = [psum.tile([P, PACK, CHUNK], F32, name="lb%d" % k, tag="bank%d" % (PACK + k)) for k in range(CHUNKS)]
         for o in range(PASSES):
@@ -214,10 +222,10 @@ def tile_picked_ysampso_wres_p_kernel(
             hcols = slice(part * CHUNK, (part + 1) * CHUNK)
             lb_sq[k] = keep.tile([P, PACK, CHUNK], F32, name="lb_sq%d" % k)
             term_b[k] = keep.tile([P, PACK, CHUNK], F32, name="term_b%d" % k)
-            if k < 2:
+            if k < 4:
                 nc.vector.tensor_tensor(term_b[k][:], lb[k][:], u2_sb[h][:, :, hcols], ALU.mult)
             nc.scalar.activation(lb_sq[k][:], lb[k][:], ACT.Square)
-            if k >= 2:
+            if k >= 4:
                 nc.vector.tensor_tensor(term_b[k][:], lb[k][:], u2_sb[h][:, :, hcols], ALU.mult)
 
         def front(i):
@@ -232,7 +240,7 @@ def tile_picked_ysampso_wres_p_kernel(
             den = work.tile([P, PACK, width], F32, name="den")
             alg[i] = keep.tile([P, PACK, width], F32, name="alg%d" % i)
             inv_root[i] = work.tile([P, PACK, width], F32, name="inv_root")
-            nc.vector.tensor_tensor(grad[:], lb_sq[k][:, :, kcols], grad_a[:, :, cols], ALU.add)
+            nc.vector.tensor_tensor(grad[:], lb_sq[k][:, :, kcols], grad_a[h][:, :, hcols], ALU.add)
             for t in range(PACK):
                 nc.vector.scalar_tensor_tensor(
                     alg[i][:, t, :], term_b[k][:, t, kcols], unit_sb[:, t : t + 1], term_a[:, t, cols],
@@ -268,7 +276,7 @@ def tile_picked_ysampso_wres_p_kernel(
             nc.vector.quantize_mx(
                 out=hid_codes[:].bitcast(FP8X4), scales=hid_exps[:], in_=hid[:].rearrange("p n t -> p (n t)")
             )
-            acc = psum.tile([P, N // P, width], F32, name="acc%d" % i, tag="bank%d" % (i % PACK))
+            acc = psum.tile([P, N // P, width], F32, name="acc%d" % i, tag="bank%d" % (PACK + i % PACK))
             for g in range(N // P):
                 m = slice(g * P, (g + 1) * P)
                 nc.tensor.matmul_mx(
@@ -284,21 +292,25 @@ def tile_picked_ysampso_wres_p_kernel(
             nc.scalar.copy(result[:], acc[:])
             nc.sync.dma_start(out[:, lo:hi].rearrange("(g m) j -> m g j", m=P), result[:])
 
+        weigh_la(0)
         read_lb(0)
         read_lb(1)
         front(0)
-        middle(0)
-        read_lb(2)
         front(1)
-        quantize_w3()
-        middle(1)
+        middle(0)
+        fetch_partner(1)
+        add_partner(1)
+        weigh_la(1)
+        read_lb(2)
         read_lb(3)
+        middle(1)
         front(2)
-        middle(2)
         front(3)
-        middle(3)
+        middle(2)
         front(4)
+        middle(3)
         middle(4)
+        quantize_w3()
         back(0)
         back(1)
         back(2)

@@ -1,6 +1,7 @@
 from contextlib import ExitStack
 
 import concourse.mybir as mybir
+from concourse.masks import make_identity
 
 K, T, S, N, H = 1024, 1024, 512, 256, 512
 FLOPS = 2 * (2 * K * H * S + H * N * S)
@@ -19,9 +20,14 @@ P = 128
 PACK = 4
 K_PASS = P * PACK
 PASSES = K // K_PASS
+QUADRANT = 32
+LIST_ROWS = 16
+LINE = 4
+HALF = S // 2
 CHUNK = 128
 CHUNKS = S // CHUNK
-HALF = S // 2
+BANKS = 8
+PIECES = [(0, 128), (128, 256), (256, 384), (384, 448), (448, 512)]
 
 
 def tile_picked_ysampso_wres_p_kernel(
@@ -34,13 +40,17 @@ def tile_picked_ysampso_wres_p_kernel(
         work = ctx.enter_context(tc.tile_pool(name="work", bufs=3))
         psum = ctx.enter_context(tc.psum_pool(name="psum", bufs=1))
 
-        offs_sb = lists.tile([P, S // 16], U16, name="offs_sb")
-        mod_sb = lists.tile([P, S // 16], U16, name="mod_sb")
-
+        offs_sb = lists.tile([P, S // LIST_ROWS], U16, name="offs_sb")
+        mod_sb = lists.tile([P, S // LIST_ROWS], U16, name="mod_sb")
         table_words = [keep.tile([P, T], U32, name="table_words%d" % o, align_bytes=64) for o in range(PASSES)]
-        w_raw = [
-            [keep.tile([P, PACK, H], F32, name="w_raw%d_%d" % (a, o), tag="w_raw%d_%d" % (a, o)) for o in range(PASSES)] for a in range(2)
-        ]
+        landed_scales = keep.tile([P, T], U8, name="landed_scales", align_bytes=64)
+        table_scales = keep.tile([P, T], U8, name="table_scales", align_bytes=64)
+        w_raw = [[keep.tile([P, PACK, H], F32, name="w_raw%d_%d" % (a, o)) for o in range(PASSES)] for a in range(2)]
+        unit_sb = keep.tile([P, PACK], F32, name="unit_sb")
+        u1_sb = [keep.tile([P, PACK, HALF], F32, name="u1_sb%d" % h) for h in range(2)]
+        u2_sb = [keep.tile([P, PACK, HALF], F32, name="u2_sb%d" % h) for h in range(2)]
+        thr_sb = [keep.tile([P, PACK, HALF], F32, name="thr_sb%d" % h) for h in range(2)]
+        w3_raw = keep.tile([P, PACK, N], F32, name="w3_raw")
 
         def load_table(o):
             nc.sync.dma_start(
@@ -51,31 +61,16 @@ def tile_picked_ysampso_wres_p_kernel(
             rows = w[o * K_PASS : (o + 1) * K_PASS, :]
             nc.sync.dma_start(w_raw[a][o][:], rows.rearrange("(p j) c -> p j c", j=PACK))
 
-        u1_sb = [keep.tile([P, PACK, HALF], F32, name="u1_sb%d" % h) for h in range(2)]
-        u2_sb = [keep.tile([P, PACK, HALF], F32, name="u2_sb%d" % h) for h in range(2)]
-        thr_sb = [keep.tile([P, PACK, HALF], F32, name="thr_sb%d" % h) for h in range(2)]
-        w3_raw = keep.tile([P, PACK, N], F32, name="w3_raw")
-
         def load_half(tiles, src, h):
             cols = slice(h * HALF, (h + 1) * HALF)
             nc.sync.dma_start(tiles[h][:], src[:, cols].rearrange("(p t) j -> p t j", t=PACK))
 
+        scale_rows = [slice(q * QUADRANT, q * QUADRANT + 4 * PASSES) for q in range(P // QUADRANT)]
         load_table(0)
-        unit_sb = keep.tile([P, PACK], F32, name="unit_sb")
         nc.sync.dma_start(unit_sb[:], unit.rearrange("(p t) o -> p (t o)", t=PACK))
         nc.sync.dma_start(offs_sb[:], offs)
-
-        table_scales = keep.tile([P, T], U8, name="table_scales", align_bytes=64)
-        landed_scales = keep.tile([P, T], U8, name="landed_scales", align_bytes=64)
-        nc.vector.memset(table_scales[:].bitcast(I32), 0)
-        for quad in range(4):
-            rows = slice(32 * quad, 32 * quad + 4 * PASSES)
-            nc.sync.dma_start(
-                landed_scales[rows, :].bitcast(I32), x_scales[:, 4 * quad : 4 * quad + 4, :].bitcast(I32)
-            )
-        for quad in range(4):
-            rows = slice(32 * quad, 32 * quad + 4 * PASSES)
-            nc.vector.tensor_copy(table_scales[rows, :].bitcast(I32), landed_scales[rows, :].bitcast(I32))
+        for q, rows in enumerate(scale_rows):
+            nc.sync.dma_start(landed_scales[rows, :].bitcast(I32), x_scales[:, 4 * q : 4 * q + 4, :].bitcast(I32))
         load_weight(0, w1, 0)
         load_table(1)
         load_weight(0, w1, 1)
@@ -83,12 +78,15 @@ def tile_picked_ysampso_wres_p_kernel(
         load_weight(1, w2, 0)
         load_weight(1, w2, 1)
         load_half(u1_sb, u1, 0)
-        load_half(u2_sb, u2, 0)
-        load_half(thr_sb, thr, 0)
         load_half(u1_sb, u1, 1)
-        load_half(u2_sb, u2, 1)
-        load_half(thr_sb, thr, 1)
+        for h in range(2):
+            load_half(u2_sb, u2, h)
+            load_half(thr_sb, thr, h)
         nc.sync.dma_start(w3_raw[:], w3.rearrange("(p j) c -> p j c", j=PACK))
+
+        nc.vector.memset(table_scales[:].bitcast(I32), 0)
+        for rows in scale_rows:
+            nc.vector.tensor_copy(table_scales[rows, :].bitcast(I32), landed_scales[rows, :].bitcast(I32))
 
         unit_safe = keep.tile([P, PACK], F32, name="unit_safe")
         unit_root = keep.tile([P, PACK], F32, name="unit_root")
@@ -98,10 +96,9 @@ def tile_picked_ysampso_wres_p_kernel(
         unit_inv = keep.tile([P, PACK], F32, name="unit_inv")
         nc.vector.scalar_tensor_tensor(unit_safe[:], unit_sb[:], 0.0, unit_sb[:], ALU.is_equal, ALU.add)
         nc.scalar.activation(unit_root[:], unit_safe[:], ACT.Abs_reciprocal_sqrt)
-        nc.vector.tensor_tensor(unit_guess[:], unit_root[:], unit_root[:], ALU.mult)
-        nc.vector.tensor_tensor(unit_err[:], unit_guess[:], unit_safe[:], ALU.mult)
-        nc.vector.scalar_tensor_tensor(unit_fix[:], unit_err[:], -0.5, unit_err[:], ALU.mult, ALU.mult)
-        nc.vector.scalar_tensor_tensor(unit_inv[:], unit_fix[:], 1.5, unit_guess[:], ALU.add, ALU.mult)
+
+        ident = keep.tile([P, P], F32, name="ident")
+        make_identity(nc, ident[:])
 
         x_codes = [keep.tile([P, S], U32, name="x_codes%d" % o, align_bytes=64) for o in range(PASSES)]
         x_exps = keep.tile([P, S], U8, name="x_exps", align_bytes=64)
@@ -109,178 +106,157 @@ def tile_picked_ysampso_wres_p_kernel(
         nc.vector.tensor_copy(x_exps[:], table_scales[:].indirect(offs_sb[:]))
         nc.vector.tensor_copy(x_codes[1][:], table_words[1][:].indirect(offs_sb[:]))
 
-        w_codes = [[None] * PASSES for a in range(2)]
-        w_exps = [[None] * PASSES for a in range(2)]
-
-        def quantize_weight(a, o, casters):
-            pairs = []
-            for u in range(2):
-                grouped = keep.tile([P, 2, P, PACK], BF16, name="w_bf%d_%d_%d" % (a, o, u), align_bytes=64)
-                src = w_raw[a][o][:].rearrange("p j (m t) -> p m j t", t=PACK)[:, :, :, 2 * u : 2 * u + 2]
-                casters[u](grouped[:].rearrange("p t m j -> p m j t"), src)
-                pairs.append(grouped)
-            codes, exps = [], []
-            for u in range(2):
-                c = keep.tile([P, 2 * P], U32, name="w_codes%d_%d_%d" % (a, o, u), align_bytes=64)
-                e = keep.tile([P, 2 * P], U8, name="w_exps%d_%d_%d" % (a, o, u), align_bytes=64)
-                nc.vector.quantize_mx(
-                    out=c[:].bitcast(FP8X4), scales=e[:], in_=pairs[u][:].rearrange("p t m j -> p (t m j)")
-                )
-                codes.append(c)
-                exps.append(e)
-            w_codes[a][o] = codes
-            w_exps[a][o] = exps
-
-        def first_product(acc, a, o, t, cols, start, stop):
-            m = slice((t % 2) * P, (t % 2 + 1) * P)
-            nc.tensor.matmul_mx(
-                out=acc,
-                lhsT=w_codes[a][o][t // 2][:, m].bitcast(FP8X4),
-                lhsT_scale=w_exps[a][o][t // 2][:, m],
-                rhs=x_codes[o][:, cols].bitcast(FP8X4),
-                rhs_scale=x_exps[4 * o : P, cols],
-                start=start,
-                stop=stop,
-            )
+        def first_product(a, casters):
+            acc = [psum.tile([P, S], F32, name="acc%d_%d" % (a, t), tag="bank%d" % (PACK * a + t)) for t in range(PACK)]
+            for o in range(PASSES):
+                grouped = []
+                for pair in range(2):
+                    rounded = keep.tile([P, 2, P, PACK], BF16, name="w_bf%d_%d_%d" % (a, o, pair), align_bytes=64)
+                    dealt = w_raw[a][o][:].rearrange("p j (m t) -> p m j t", t=PACK)[:, :, :, 2 * pair : 2 * pair + 2]
+                    casters[o][pair](rounded[:].rearrange("p t m j -> p m j t"), dealt)
+                    grouped.append(rounded)
+                for pair in range(2):
+                    codes = keep.tile([P, 2 * P], U32, name="w_codes%d_%d_%d" % (a, o, pair), align_bytes=64)
+                    exps = keep.tile([P, 2 * P], U8, name="w_exps%d_%d_%d" % (a, o, pair), align_bytes=64)
+                    nc.vector.quantize_mx(
+                        out=codes[:].bitcast(FP8X4), scales=exps[:], in_=grouped[pair][:].rearrange("p t m j -> p (t m j)")
+                    )
+                    for slot in range(2):
+                        m = slice(slot * P, (slot + 1) * P)
+                        nc.tensor.matmul_mx(
+                            out=acc[2 * pair + slot][:],
+                            lhsT=codes[:, m].bitcast(FP8X4),
+                            lhsT_scale=exps[:, m],
+                            rhs=x_codes[o][:].bitcast(FP8X4),
+                            rhs_scale=x_exps[4 * o : P, :],
+                            start=o == 0,
+                            stop=o == PASSES - 1,
+                        )
+            return acc
 
         on_scalar, on_vector = nc.scalar.copy, nc.vector.tensor_copy
-        quantize_weight(0, 0, (on_scalar, on_scalar))
-        quantize_weight(0, 1, (on_vector, on_scalar))
-
-
-        la = [psum.tile([P, S], F32, name="la%d" % t, tag="bank%d" % t) for t in range(PACK)]
-        for o in range(PASSES):
-            for t in range(PACK):
-                first_product(la[t][:], 0, o, t, slice(0, S), o == 0, o == PASSES - 1)
-
-        la_sq = [keep.tile([P, S], F32, name="la_sq%d" % t) for t in range(PACK)]
-        lm_sq = {}
-        term_a = keep.tile([P, PACK, S], F32, name="term_a")
-
+        la = first_product(0, ((on_scalar, on_scalar), (on_vector, on_scalar)))
+        la_sq = keep.tile([P, PACK, S], F32, name="la_sq")
         for t in range(PACK):
-            nc.scalar.activation(la_sq[t][:], la[t][:], ACT.Square)
+            nc.scalar.activation(la_sq[:, t, :], la[t][:], ACT.Square)
 
-        def weigh_la(h):
-            cols = slice(h * HALF, (h + 1) * HALF)
+        list_cols = HALF // LIST_ROWS
+        partner = [keep.tile([P, PACK, HALF], F32, name="partner%d" % h) for h in range(2)]
+        for h in range(2):
+            for t in range(PACK):
+                window = la_sq[:, t, :].indirect(mod_sb[:, h * list_cols : (h + 1) * list_cols])
+                nc.scalar.activation(partner[h][:, t, :], window, ACT.Copy, scale=0.5)
+
+        nc.vector.tensor_tensor(unit_guess[:], unit_root[:], unit_root[:], ALU.mult)
+        nc.vector.tensor_tensor(unit_err[:], unit_guess[:], unit_safe[:], ALU.mult)
+        nc.vector.scalar_tensor_tensor(unit_fix[:], unit_err[:], -0.5, unit_err[:], ALU.mult, ALU.mult)
+        nc.vector.scalar_tensor_tensor(unit_inv[:], unit_fix[:], 1.5, unit_guess[:], ALU.add, ALU.mult)
+
+        lb = first_product(1, ((on_vector, on_vector), (on_vector, on_vector)))
+
+        term_a = [keep.tile([P, PACK, HALF], F32, name="term_a%d" % h) for h in range(2)]
+        term_b = [keep.tile([P, PACK, HALF], F32, name="term_b%d" % h) for h in range(2)]
+        lb_sq = [keep.tile([P, PACK, HALF], F32, name="lb_sq%d" % h) for h in range(2)]
+        thr_root = [keep.tile([P, PACK, HALF], F32, name="thr_root%d" % h) for h in range(2)]
+
+        def weigh(terms, acc, coords, h):
             for t in range(PACK):
                 nc.vector.scalar_tensor_tensor(
-                    term_a[:, t, cols], la[t][:, cols], unit_sb[:, t : t + 1], u1_sb[h][:, t, :], ALU.mult, ALU.mult
+                    terms[h][:, t, :], acc[t][:, h * HALF : (h + 1) * HALF], unit_sb[:, t : t + 1], coords[h][:, t, :],
+                    ALU.mult, ALU.mult,
                 )
 
-        def fetch_partner(h):
-            cols = slice(h * HALF, (h + 1) * HALF)
+        def square_lb(h):
             for t in range(PACK):
-                lm_sq[h, t] = keep.tile([P, HALF], F32, name="lm_sq%d_%d" % (h, t), tag="lm_%d" % t)
-                nc.scalar.activation(
-                    lm_sq[h, t][:], la_sq[t][:].indirect(mod_sb[:, 16 * h : 16 * (h + 1)]), ACT.Copy, scale=0.5
-                )
+                nc.scalar.activation(lb_sq[h][:, t, :], lb[t][:, h * HALF : (h + 1) * HALF], ACT.Square)
 
-        grad_a = {}
+        def root_thr(h):
+            nc.scalar.activation(thr_root[h][:], thr_sb[h][:], ACT.Abs_reciprocal_sqrt)
 
-        def add_partner(h):
-            cols = slice(h * HALF, (h + 1) * HALF)
-            grad_a[h] = keep.tile([P, PACK, HALF], F32, name="grad_a%d" % h, tag=("w_raw1_1","thr_sb0")[h])
-            for t in range(PACK):
-                adder = nc.gpsimd if True else nc.vector
-                adder.tensor_tensor(grad_a[h][:, t, :], lm_sq[h, t][:], la_sq[t][:, cols], ALU.add)
+        sum_banks = 3
+        grad_root = {}
 
-        fetch_partner(0)
-        quantize_weight(1, 0, (on_vector, on_vector))
-        quantize_weight(1, 1, (on_vector, on_vector))
-        add_partner(0)
-
-        lb = [psum.tile([P, PACK, CHUNK], F32, name="lb%d" % k, tag="bank%d" % (PACK + k)) for k in range(CHUNKS)]
-        for o in range(PASSES):
-            for k in range(CHUNKS):
+        def root_grad(k):
+            h, part = divmod(k, 2)
+            cols = slice(k * CHUNK, (k + 1) * CHUNK)
+            half_cols = slice(part * CHUNK, (part + 1) * CHUNK)
+            grad_t = psum.tile([P, PACK, P], F32, name="grad_t%d" % k, tag="bank%d" % (k % sum_banks))
+            squares = [la_sq[:, :, cols], partner[h][:, :, half_cols], lb_sq[h][:, :, half_cols]]
+            for n, square in enumerate(squares):
                 for t in range(PACK):
-                    first_product(
-                        lb[k][:, t, :], 1, o, t, slice(k * CHUNK, (k + 1) * CHUNK),
-                        o == 0 and t == 0, o == PASSES - 1 and t == PACK - 1,
+                    nc.tensor.matmul(
+                        grad_t[:, t, :], lhsT=square[:, t, :], rhs=ident[:], is_transpose=True,
+                        start=n == 0 and t == 0, stop=n == len(squares) - 1 and t == PACK - 1,
                     )
+            root_t = work.tile([P, PACK, P], F32, name="root_t")
+            nc.scalar.activation(root_t[:], grad_t[:], ACT.Abs_reciprocal_sqrt, bias=0.3)
+            grad_root[k] = psum.tile([P, PACK, CHUNK], F32, name="grad_root%d" % k, tag="bank%d" % (sum_banks + k))
+            for t in range(PACK):
+                nc.tensor.transpose(grad_root[k][:, t, :], root_t[:, t, :], ident[:])
+
+        alg, scaled, factors = {}, {}, {}
+
+        def add_terms(k):
+            h, part = divmod(k, 2)
+            cols = slice(part * CHUNK, (part + 1) * CHUNK)
+            alg[k] = keep.tile([P, PACK, CHUNK], F32, name="alg%d" % k)
+            scaled[k] = keep.tile([P, PACK, CHUNK], F32, name="scaled%d" % k)
+            nc.vector.tensor_tensor(alg[k][:], term_a[h][:, :, cols], term_b[h][:, :, cols], ALU.add)
+            nc.vector.tensor_tensor(scaled[k][:], alg[k][:], thr_root[h][:, :, cols], ALU.mult)
+
+        def weight(i):
+            lo, hi = PIECES[i]
+            width = hi - lo
+            k = lo // CHUNK
+            cols = slice(lo - k * CHUNK, hi - k * CHUNK)
+            ratio = work.tile([P, PACK, width], F32, name="ratio")
+            ratio_sq = work.tile([P, PACK, width], F32, name="ratio_sq")
+            gm_root = keep.tile([P, PACK, width], F32, name="gm_root%d" % i)
+            product = keep.tile([P, PACK, width], F32, name="product%d" % i)
+            nc.vector.tensor_tensor(ratio[:], grad_root[k][:, :, cols], scaled[k][:, :, cols], ALU.mult)
+            for t in range(PACK):
+                nc.scalar.activation(ratio_sq[:, t, :], ratio[:, t, :], ACT.Square, scale=unit_inv[:, t : t + 1])
+            nc.scalar.activation(gm_root[:], ratio_sq[:], ACT.Abs_reciprocal_sqrt, bias=1.0)
+            if k == CHUNKS - 1:
+                nc.scalar.activation(product[:], gm_root[:], ACT.Square)
+                factors[i] = (alg[k][:, :, cols], product[:])
+            else:
+                nc.vector.tensor_tensor(product[:], alg[k][:, :, cols], gm_root[:], ALU.mult)
+                factors[i] = (gm_root[:], product[:])
 
         w3_bf = keep.tile([P, N, PACK], BF16, name="w3_bf", align_bytes=64)
         w3_codes = keep.tile([P, N], U32, name="w3_codes", align_bytes=64)
         w3_exps = keep.tile([P, N], U8, name="w3_exps", align_bytes=64)
 
         def quantize_w3():
-            nc.scalar.copy(
-                w3_bf[:].rearrange("p (c i) j -> p c j i", i=4), w3_raw[:].rearrange("p j (c i) -> p c j i", i=4)
+            nc.vector.tensor_copy(
+                w3_bf[:].rearrange("p (c i) j -> p c j i", i=LINE), w3_raw[:].rearrange("p j (c i) -> p c j i", i=LINE)
             )
             nc.vector.quantize_mx(
                 out=w3_codes[:].bitcast(FP8X4), scales=w3_exps[:], in_=w3_bf[:].rearrange("p n j -> p (n j)")
             )
 
-        pieces = [(0,128),(128,256),(256,384),(384,448),(448,512)]
-        term_b = {}
-        lb_sq = {}
-        alg = {}
-        inv_root = {}
-        gm = {}
-
-        def read_lb(k):
-            h, part = divmod(k, 2)
-            hcols = slice(part * CHUNK, (part + 1) * CHUNK)
-            lb_sq[k] = keep.tile([P, PACK, CHUNK], F32, name="lb_sq%d" % k)
-            term_b[k] = keep.tile([P, PACK, CHUNK], F32, name="term_b%d" % k)
-            if k < 4:
-                nc.vector.tensor_tensor(term_b[k][:], lb[k][:], u2_sb[h][:, :, hcols], ALU.mult)
-            nc.scalar.activation(lb_sq[k][:], lb[k][:], ACT.Square)
-            if k >= 4:
-                nc.vector.tensor_tensor(term_b[k][:], lb[k][:], u2_sb[h][:, :, hcols], ALU.mult)
-
-        def front(i):
-            lo, hi = pieces[i]
-            width = hi - lo
-            cols = slice(lo, hi)
-            k = lo // CHUNK
-            kcols = slice(lo - k * CHUNK, hi - k * CHUNK)
-            h = lo // HALF
-            hcols = slice(lo - h * HALF, hi - h * HALF)
-            grad = work.tile([P, PACK, width], F32, name="grad")
-            den = work.tile([P, PACK, width], F32, name="den")
-            alg[i] = keep.tile([P, PACK, width], F32, name="alg%d" % i)
-            inv_root[i] = work.tile([P, PACK, width], F32, name="inv_root")
-            nc.vector.tensor_tensor(grad[:], lb_sq[k][:, :, kcols], grad_a[h][:, :, hcols], ALU.add)
-            for t in range(PACK):
-                nc.vector.scalar_tensor_tensor(
-                    alg[i][:, t, :], term_b[k][:, t, kcols], unit_sb[:, t : t + 1], term_a[:, t, cols],
-                    ALU.mult, ALU.add,
-                )
-            nc.vector.scalar_tensor_tensor(den[:], grad[:], 0.3, thr_sb[h][:, :, hcols], ALU.add, ALU.mult)
-            nc.scalar.activation(inv_root[i][:], den[:], ACT.Abs_reciprocal_sqrt)
-
-        def middle(i):
-            width = pieces[i][1] - pieces[i][0]
-            ratio = work.tile([P, PACK, width], F32, name="ratio")
-            ratio_sq = work.tile([P, PACK, width], F32, name="ratio_sq")
-            gm_root = work.tile([P, PACK, width], F32, name="gm_root")
-            gm[i] = work.tile([P, PACK, width], F32, name="gm")
-            nc.vector.tensor_tensor(ratio[:], alg[i][:], inv_root[i][:], ALU.mult)
-            for t in range(PACK):
-                nc.scalar.activation(ratio_sq[:, t, :], ratio[:, t, :], ACT.Square, scale=unit_inv[:, t : t + 1])
-            nc.scalar.activation(gm_root[:], ratio_sq[:], ACT.Abs_reciprocal_sqrt, bias=1.0)
-            nc.scalar.activation(gm[i][:], gm_root[:], ACT.Square)
-
-        def back(i):
-            lo, hi = pieces[i]
+        def mix(i):
+            lo, hi = PIECES[i]
             width = hi - lo
             hid = work.tile([P, width, PACK], BF16, name="hid", align_bytes=64)
             hid_codes = work.tile([P, width], U32, name="hid_codes", align_bytes=64)
             hid_exps = work.tile([P, width], U8, name="hid_exps", align_bytes=64)
             nc.vector.tensor_tensor(
-                hid[:].rearrange("p (c i) t -> p c t i", i=4),
-                alg[i][:].rearrange("p t (c i) -> p c t i", i=4),
-                gm[i][:].rearrange("p t (c i) -> p c t i", i=4),
+                hid[:].rearrange("p (c i) t -> p c t i", i=LINE),
+                factors[i][0].rearrange("p t (c i) -> p c t i", i=LINE),
+                factors[i][1].rearrange("p t (c i) -> p c t i", i=LINE),
                 ALU.mult,
             )
             nc.vector.quantize_mx(
                 out=hid_codes[:].bitcast(FP8X4), scales=hid_exps[:], in_=hid[:].rearrange("p n t -> p (n t)")
             )
-            acc = psum.tile([P, N // P, width], F32, name="acc%d" % i, tag="bank%d" % (PACK + i % PACK))
+            bank = (sum_banks + CHUNKS + i) % BANKS
+            mixed = psum.tile([P, N // P, width], F32, name="mixed%d" % i, tag="bank%d" % bank)
             for g in range(N // P):
                 m = slice(g * P, (g + 1) * P)
                 nc.tensor.matmul_mx(
-                    out=acc[:, g, :],
+                    out=mixed[:, g, :],
                     lhsT=w3_codes[:, m].bitcast(FP8X4),
                     lhsT_scale=w3_exps[:, m],
                     rhs=hid_codes[:].bitcast(FP8X4),
@@ -288,31 +264,29 @@ def tile_picked_ysampso_wres_p_kernel(
                     start=True,
                     stop=True,
                 )
-            result = work.tile([P, N // P, width], F32, name="result")
-            nc.scalar.copy(result[:], acc[:])
+            result = keep.tile([P, N // P, width], F32, name="result%d" % i)
+            nc.scalar.copy(result[:], mixed[:])
             nc.sync.dma_start(out[:, lo:hi].rearrange("(g m) j -> m g j", m=P), result[:])
 
-        weigh_la(0)
-        read_lb(0)
-        read_lb(1)
-        front(0)
-        front(1)
-        middle(0)
-        fetch_partner(1)
-        add_partner(1)
-        weigh_la(1)
-        read_lb(2)
-        read_lb(3)
-        middle(1)
-        front(2)
-        front(3)
-        middle(2)
-        front(4)
-        middle(3)
-        middle(4)
+        weigh(term_a, la, u1_sb, 0)
+        weigh(term_a, la, u1_sb, 1)
+        weigh(term_b, lb, u2_sb, 0)
+        square_lb(0)
+        square_lb(1)
+        weigh(term_b, lb, u2_sb, 1)
+
+        root_thr(0)
+        root_grad(0)
+        for k in range(CHUNKS):
+            if (k + 1) * CHUNK == HALF:
+                root_thr(1)
+            if k + 1 < CHUNKS:
+                root_grad(k + 1)
+            add_terms(k)
+            for i, (lo, hi) in enumerate(PIECES):
+                if lo // CHUNK == k:
+                    weight(i)
+
         quantize_w3()
-        back(0)
-        back(1)
-        back(2)
-        back(3)
-        back(4)
+        for i in range(len(PIECES)):
+            mix(i)

@@ -88,27 +88,41 @@ def tile_picked_ysampso_wres_p_kernel(
         for rows in scale_rows:
             nc.vector.tensor_copy(table_scales[rows, :].bitcast(I32), landed_scales[rows, :].bitcast(I32))
 
+        unit_zero = keep.tile([P, PACK], F32, name="unit_zero")
         unit_safe = keep.tile([P, PACK], F32, name="unit_safe")
         unit_root = keep.tile([P, PACK], F32, name="unit_root")
         unit_guess = keep.tile([P, PACK], F32, name="unit_guess")
         unit_err = keep.tile([P, PACK], F32, name="unit_err")
+        unit_err_sq = keep.tile([P, PACK], F32, name="unit_err_sq")
         unit_fix = keep.tile([P, PACK], F32, name="unit_fix")
         unit_inv = keep.tile([P, PACK], F32, name="unit_inv")
-        nc.vector.scalar_tensor_tensor(unit_safe[:], unit_sb[:], 0.0, unit_sb[:], ALU.is_equal, ALU.add)
+        nc.gpsimd.tensor_single_scalar(unit_zero[:], unit_sb[:], 0.0, ALU.is_equal)
+        nc.gpsimd.tensor_tensor(unit_safe[:], unit_zero[:], unit_sb[:], ALU.add)
         nc.scalar.activation(unit_root[:], unit_safe[:], ACT.Abs_reciprocal_sqrt)
+        nc.gpsimd.tensor_tensor(unit_guess[:], unit_root[:], unit_root[:], ALU.mult)
+        nc.gpsimd.tensor_tensor(unit_err[:], unit_guess[:], unit_safe[:], ALU.mult)
+        nc.gpsimd.tensor_tensor(unit_err_sq[:], unit_err[:], unit_err[:], ALU.mult)
+        nc.gpsimd.tensor_scalar(unit_fix[:], unit_err_sq[:], -0.5, 1.5, ALU.mult, ALU.add)
+        nc.gpsimd.tensor_tensor(unit_inv[:], unit_fix[:], unit_guess[:], ALU.mult)
 
         ident = keep.tile([P, P], F32, name="ident")
         make_identity(nc, ident[:])
 
-        x_codes = [keep.tile([P, S], U32, name="x_codes%d" % o, align_bytes=64) for o in range(PASSES)]
+        x_codes = {}
         x_exps = keep.tile([P, S], U8, name="x_exps", align_bytes=64)
-        nc.vector.tensor_copy(x_codes[0][:], table_words[0][:].indirect(offs_sb[:]))
+
+        def pick_words(o, tag):
+            x_codes[o] = keep.tile([P, S], U32, name="x_codes%d" % o, tag=tag, align_bytes=64)
+            nc.vector.tensor_copy(x_codes[o][:], table_words[o][:].indirect(offs_sb[:]))
+
+        pick_words(0, "x_codes0")
         nc.vector.tensor_copy(x_exps[:], table_scales[:].indirect(offs_sb[:]))
-        nc.vector.tensor_copy(x_codes[1][:], table_words[1][:].indirect(offs_sb[:]))
 
         def first_product(a, casters):
             acc = [psum.tile([P, S], F32, name="acc%d_%d" % (a, t), tag="bank%d" % (PACK * a + t)) for t in range(PACK)]
             for o in range(PASSES):
+                if o not in x_codes:
+                    pick_words(o, "w_bf0_0_0")
                 grouped = []
                 for pair in range(2):
                     rounded = keep.tile([P, 2, P, PACK], BF16, name="w_bf%d_%d_%d" % (a, o, pair), align_bytes=64)
@@ -146,11 +160,6 @@ def tile_picked_ysampso_wres_p_kernel(
             for t in range(PACK):
                 window = la_sq[:, t, :].indirect(mod_sb[:, h * list_cols : (h + 1) * list_cols])
                 nc.scalar.activation(partner[h][:, t, :], window, ACT.Copy, scale=0.5)
-
-        nc.vector.tensor_tensor(unit_guess[:], unit_root[:], unit_root[:], ALU.mult)
-        nc.vector.tensor_tensor(unit_err[:], unit_guess[:], unit_safe[:], ALU.mult)
-        nc.vector.scalar_tensor_tensor(unit_fix[:], unit_err[:], -0.5, unit_err[:], ALU.mult, ALU.mult)
-        nc.vector.scalar_tensor_tensor(unit_inv[:], unit_fix[:], 1.5, unit_guess[:], ALU.add, ALU.mult)
 
         lb = first_product(1, ((on_vector, on_vector), (on_vector, on_vector)))
 

from contextlib import ExitStack

import concourse.mybir as mybir
from concourse.masks import make_identity

K, T, S, N, H = 1024, 1024, 512, 256, 512
FLOPS = 2 * (2 * K * H * S + H * N * S)

F32 = mybir.dt.float32
BF16 = mybir.dt.bfloat16
I32 = mybir.dt.int32
U32 = mybir.dt.uint32
U16 = mybir.dt.uint16
U8 = mybir.dt.uint8
FP8X4 = mybir.dt.float8_e4m3fn_x4
ALU = mybir.AluOpType
ACT = mybir.ActivationFunctionType

P = 128
PACK = 4
K_PASS = P * PACK
PASSES = K // K_PASS
QUADRANT = 32
LIST_ROWS = 16
LINE = 4
HALF = S // 2
CHUNK = 128
CHUNKS = S // CHUNK
BANKS = 8
PIECES = [(0, 128), (128, 256), (256, 384), (384, 448), (448, 512)]


def tile_picked_ysampso_wres_p_kernel(
    tc, x_words, x_scales, w1, w2, u1, u2, thr, unit, w3, offs, mod, out
):
    nc = tc.nc
    with ExitStack() as ctx:
        lists = ctx.enter_context(tc.tile_pool(name="lists", bufs=1))
        keep = ctx.enter_context(tc.tile_pool(name="keep", bufs=1))
        work = ctx.enter_context(tc.tile_pool(name="work", bufs=3))
        psum = ctx.enter_context(tc.psum_pool(name="psum", bufs=1))

        offs_sb = lists.tile([P, S // LIST_ROWS], U16, name="offs_sb")
        mod_sb = lists.tile([P, S // LIST_ROWS], U16, name="mod_sb")
        table_words = [keep.tile([P, T], U32, name="table_words%d" % o, align_bytes=64) for o in range(PASSES)]
        landed_scales = keep.tile([P, T], U8, name="landed_scales", align_bytes=64)
        table_scales = keep.tile([P, T], U8, name="table_scales", align_bytes=64)
        w_raw = [[keep.tile([P, PACK, H], F32, name="w_raw%d_%d" % (a, o)) for o in range(PASSES)] for a in range(2)]
        unit_sb = keep.tile([P, PACK], F32, name="unit_sb")
        u1_sb = [keep.tile([P, PACK, HALF], F32, name="u1_sb%d" % h) for h in range(2)]
        u2_sb = [keep.tile([P, PACK, HALF], F32, name="u2_sb%d" % h) for h in range(2)]
        thr_sb = [keep.tile([P, PACK, HALF], F32, name="thr_sb%d" % h) for h in range(2)]
        w3_raw = keep.tile([P, PACK, N], F32, name="w3_raw")

        def load_table(o):
            nc.sync.dma_start(
                table_words[o][:].bitcast(I32), x_words[o].rearrange("p n t -> p (n t)").bitcast(I32)
            )

        def load_weight(a, w, o):
            rows = w[o * K_PASS : (o + 1) * K_PASS, :]
            nc.sync.dma_start(w_raw[a][o][:], rows.rearrange("(p j) c -> p j c", j=PACK))

        def load_half(tiles, src, h):
            cols = slice(h * HALF, (h + 1) * HALF)
            nc.sync.dma_start(tiles[h][:], src[:, cols].rearrange("(p t) j -> p t j", t=PACK))

        scale_rows = [slice(q * QUADRANT, q * QUADRANT + 4 * PASSES) for q in range(P // QUADRANT)]
        load_table(0)
        nc.sync.dma_start(unit_sb[:], unit.rearrange("(p t) o -> p (t o)", t=PACK))
        nc.sync.dma_start(offs_sb[:], offs)
        for q, rows in enumerate(scale_rows):
            nc.sync.dma_start(landed_scales[rows, :].bitcast(I32), x_scales[:, 4 * q : 4 * q + 4, :].bitcast(I32))
        load_weight(0, w1, 0)
        load_table(1)
        load_weight(0, w1, 1)
        nc.sync.dma_start(mod_sb[:], mod)
        load_weight(1, w2, 0)
        load_weight(1, w2, 1)
        load_half(u1_sb, u1, 0)
        load_half(u1_sb, u1, 1)
        for h in range(2):
            load_half(u2_sb, u2, h)
            load_half(thr_sb, thr, h)
        nc.sync.dma_start(w3_raw[:], w3.rearrange("(p j) c -> p j c", j=PACK))

        nc.vector.memset(table_scales[:].bitcast(I32), 0)
        for rows in scale_rows:
            nc.vector.tensor_copy(table_scales[rows, :].bitcast(I32), landed_scales[rows, :].bitcast(I32))

        unit_zero = keep.tile([P, PACK], F32, name="unit_zero")
        unit_safe = keep.tile([P, PACK], F32, name="unit_safe")
        unit_root = keep.tile([P, PACK], F32, name="unit_root")
        unit_guess = keep.tile([P, PACK], F32, name="unit_guess")
        unit_err = keep.tile([P, PACK], F32, name="unit_err")
        unit_err_sq = keep.tile([P, PACK], F32, name="unit_err_sq")
        unit_fix = keep.tile([P, PACK], F32, name="unit_fix")
        unit_inv = keep.tile([P, PACK], F32, name="unit_inv")
        nc.gpsimd.tensor_single_scalar(unit_zero[:], unit_sb[:], 0.0, ALU.is_equal)
        nc.gpsimd.tensor_tensor(unit_safe[:], unit_zero[:], unit_sb[:], ALU.add)
        nc.scalar.activation(unit_root[:], unit_safe[:], ACT.Abs_reciprocal_sqrt)
        nc.gpsimd.tensor_tensor(unit_guess[:], unit_root[:], unit_root[:], ALU.mult)
        nc.gpsimd.tensor_tensor(unit_err[:], unit_guess[:], unit_safe[:], ALU.mult)
        nc.gpsimd.tensor_tensor(unit_err_sq[:], unit_err[:], unit_err[:], ALU.mult)
        nc.gpsimd.tensor_scalar(unit_fix[:], unit_err_sq[:], -0.5, 1.5, ALU.mult, ALU.add)
        nc.gpsimd.tensor_tensor(unit_inv[:], unit_fix[:], unit_guess[:], ALU.mult)

        ident = keep.tile([P, P], F32, name="ident")
        make_identity(nc, ident[:])

        x_codes = {}
        x_exps = keep.tile([P, S], U8, name="x_exps", align_bytes=64)

        def pick_words(o, tag):
            x_codes[o] = keep.tile([P, S], U32, name="x_codes%d" % o, tag=tag, align_bytes=64)
            nc.vector.tensor_copy(x_codes[o][:], table_words[o][:].indirect(offs_sb[:]))

        pick_words(0, "x_codes0")
        nc.vector.tensor_copy(x_exps[:], table_scales[:].indirect(offs_sb[:]))

        def first_product(a, casters):
            acc = [psum.tile([P, S], F32, name="acc%d_%d" % (a, t), tag="bank%d" % (PACK * a + t)) for t in range(PACK)]
            for o in range(PASSES):
                if o not in x_codes:
                    pick_words(o, "w_bf0_0_0")
                grouped = []
                for pair in range(2):
                    rounded = keep.tile([P, 2, P, PACK], BF16, name="w_bf%d_%d_%d" % (a, o, pair), align_bytes=64)
                    dealt = w_raw[a][o][:].rearrange("p j (m t) -> p m j t", t=PACK)[:, :, :, 2 * pair : 2 * pair + 2]
                    casters[o][pair](rounded[:].rearrange("p t m j -> p m j t"), dealt)
                    grouped.append(rounded)
                for pair in range(2):
                    codes = keep.tile([P, 2 * P], U32, name="w_codes%d_%d_%d" % (a, o, pair), align_bytes=64)
                    exps = keep.tile([P, 2 * P], U8, name="w_exps%d_%d_%d" % (a, o, pair), align_bytes=64)
                    nc.vector.quantize_mx(
                        out=codes[:].bitcast(FP8X4), scales=exps[:], in_=grouped[pair][:].rearrange("p t m j -> p (t m j)")
                    )
                    for slot in range(2):
                        m = slice(slot * P, (slot + 1) * P)
                        nc.tensor.matmul_mx(
                            out=acc[2 * pair + slot][:],
                            lhsT=codes[:, m].bitcast(FP8X4),
                            lhsT_scale=exps[:, m],
                            rhs=x_codes[o][:].bitcast(FP8X4),
                            rhs_scale=x_exps[4 * o : P, :],
                            start=o == 0,
                            stop=o == PASSES - 1,
                        )
            return acc

        on_scalar, on_vector = nc.scalar.copy, nc.vector.tensor_copy
        la = first_product(0, ((on_scalar, on_scalar), (on_vector, on_scalar)))
        la_sq = keep.tile([P, PACK, S], F32, name="la_sq")
        for t in range(PACK):
            nc.scalar.activation(la_sq[:, t, :], la[t][:], ACT.Square)

        list_cols = HALF // LIST_ROWS
        partner = [keep.tile([P, PACK, HALF], F32, name="partner%d" % h) for h in range(2)]
        for h in range(2):
            for t in range(PACK):
                window = la_sq[:, t, :].indirect(mod_sb[:, h * list_cols : (h + 1) * list_cols])
                nc.scalar.activation(partner[h][:, t, :], window, ACT.Copy, scale=0.5)

        lb = first_product(1, ((on_vector, on_vector), (on_vector, on_vector)))

        term_a = [keep.tile([P, PACK, HALF], F32, name="term_a%d" % h) for h in range(2)]
        term_b = [keep.tile([P, PACK, HALF], F32, name="term_b%d" % h) for h in range(2)]
        lb_sq = [keep.tile([P, PACK, HALF], F32, name="lb_sq%d" % h) for h in range(2)]
        thr_root = [keep.tile([P, PACK, HALF], F32, name="thr_root%d" % h) for h in range(2)]

        def weigh(terms, acc, coords, h):
            for t in range(PACK):
                nc.vector.scalar_tensor_tensor(
                    terms[h][:, t, :], acc[t][:, h * HALF : (h + 1) * HALF], unit_sb[:, t : t + 1], coords[h][:, t, :],
                    ALU.mult, ALU.mult,
                )

        def square_lb(h):
            for t in range(PACK):
                nc.scalar.activation(lb_sq[h][:, t, :], lb[t][:, h * HALF : (h + 1) * HALF], ACT.Square)

        def root_thr(h):
            nc.scalar.activation(thr_root[h][:], thr_sb[h][:], ACT.Abs_reciprocal_sqrt)

        sum_banks = 3
        grad_root = {}

        def root_grad(k):
            h, part = divmod(k, 2)
            cols = slice(k * CHUNK, (k + 1) * CHUNK)
            half_cols = slice(part * CHUNK, (part + 1) * CHUNK)
            grad_t = psum.tile([P, PACK, P], F32, name="grad_t%d" % k, tag="bank%d" % (k % sum_banks))
            squares = [la_sq[:, :, cols], partner[h][:, :, half_cols], lb_sq[h][:, :, half_cols]]
            for n, square in enumerate(squares):
                for t in range(PACK):
                    nc.tensor.matmul(
                        grad_t[:, t, :], lhsT=square[:, t, :], rhs=ident[:], is_transpose=True,
                        start=n == 0 and t == 0, stop=n == len(squares) - 1 and t == PACK - 1,
                    )
            root_t = work.tile([P, PACK, P], F32, name="root_t")
            nc.scalar.activation(root_t[:], grad_t[:], ACT.Abs_reciprocal_sqrt, bias=0.3)
            grad_root[k] = psum.tile([P, PACK, CHUNK], F32, name="grad_root%d" % k, tag="bank%d" % (sum_banks + k))
            for t in range(PACK):
                nc.tensor.transpose(grad_root[k][:, t, :], root_t[:, t, :], ident[:])

        alg, scaled, factors = {}, {}, {}

        def add_terms(k):
            h, part = divmod(k, 2)
            cols = slice(part * CHUNK, (part + 1) * CHUNK)
            alg[k] = keep.tile([P, PACK, CHUNK], F32, name="alg%d" % k)
            scaled[k] = keep.tile([P, PACK, CHUNK], F32, name="scaled%d" % k)
            nc.vector.tensor_tensor(alg[k][:], term_a[h][:, :, cols], term_b[h][:, :, cols], ALU.add)
            nc.vector.tensor_tensor(scaled[k][:], alg[k][:], thr_root[h][:, :, cols], ALU.mult)

        def weight(i):
            lo, hi = PIECES[i]
            width = hi - lo
            k = lo // CHUNK
            cols = slice(lo - k * CHUNK, hi - k * CHUNK)
            ratio = work.tile([P, PACK, width], F32, name="ratio")
            ratio_sq = work.tile([P, PACK, width], F32, name="ratio_sq")
            gm_root = keep.tile([P, PACK, width], F32, name="gm_root%d" % i)
            product = keep.tile([P, PACK, width], F32, name="product%d" % i)
            nc.vector.tensor_tensor(ratio[:], grad_root[k][:, :, cols], scaled[k][:, :, cols], ALU.mult)
            for t in range(PACK):
                nc.scalar.activation(ratio_sq[:, t, :], ratio[:, t, :], ACT.Square, scale=unit_inv[:, t : t + 1])
            nc.scalar.activation(gm_root[:], ratio_sq[:], ACT.Abs_reciprocal_sqrt, bias=1.0)
            if k == CHUNKS - 1:
                nc.scalar.activation(product[:], gm_root[:], ACT.Square)
                factors[i] = (alg[k][:, :, cols], product[:])
            else:
                nc.vector.tensor_tensor(product[:], alg[k][:, :, cols], gm_root[:], ALU.mult)
                factors[i] = (gm_root[:], product[:])

        w3_bf = keep.tile([P, N, PACK], BF16, name="w3_bf", align_bytes=64)
        w3_codes = keep.tile([P, N], U32, name="w3_codes", align_bytes=64)
        w3_exps = keep.tile([P, N], U8, name="w3_exps", align_bytes=64)

        def quantize_w3():
            nc.vector.tensor_copy(
                w3_bf[:].rearrange("p (c i) j -> p c j i", i=LINE), w3_raw[:].rearrange("p j (c i) -> p c j i", i=LINE)
            )
            nc.vector.quantize_mx(
                out=w3_codes[:].bitcast(FP8X4), scales=w3_exps[:], in_=w3_bf[:].rearrange("p n j -> p (n j)")
            )

        def mix(i):
            lo, hi = PIECES[i]
            width = hi - lo
            hid = work.tile([P, width, PACK], BF16, name="hid", align_bytes=64)
            hid_codes = work.tile([P, width], U32, name="hid_codes", align_bytes=64)
            hid_exps = work.tile([P, width], U8, name="hid_exps", align_bytes=64)
            nc.vector.tensor_tensor(
                hid[:].rearrange("p (c i) t -> p c t i", i=LINE),
                factors[i][0].rearrange("p t (c i) -> p c t i", i=LINE),
                factors[i][1].rearrange("p t (c i) -> p c t i", i=LINE),
                ALU.mult,
            )
            nc.vector.quantize_mx(
                out=hid_codes[:].bitcast(FP8X4), scales=hid_exps[:], in_=hid[:].rearrange("p n t -> p (n t)")
            )
            bank = (sum_banks + CHUNKS + i) % BANKS
            mixed = psum.tile([P, N // P, width], F32, name="mixed%d" % i, tag="bank%d" % bank)
            for g in range(N // P):
                m = slice(g * P, (g + 1) * P)
                nc.tensor.matmul_mx(
                    out=mixed[:, g, :],
                    lhsT=w3_codes[:, m].bitcast(FP8X4),
                    lhsT_scale=w3_exps[:, m],
                    rhs=hid_codes[:].bitcast(FP8X4),
                    rhs_scale=hid_exps[:],
                    start=True,
                    stop=True,
                )
            result = keep.tile([P, N // P, width], F32, name="result%d" % i)
            nc.scalar.copy(result[:], mixed[:])
            nc.sync.dma_start(out[:, lo:hi].rearrange("(g m) j -> m g j", m=P), result[:])

        weigh(term_a, la, u1_sb, 0)
        weigh(term_a, la, u1_sb, 1)
        weigh(term_b, lb, u2_sb, 0)
        square_lb(0)
        square_lb(1)
        weigh(term_b, lb, u2_sb, 1)

        root_thr(0)
        root_grad(0)
        for k in range(CHUNKS):
            if (k + 1) * CHUNK == HALF:
                root_thr(1)
            if k + 1 < CHUNKS:
                root_grad(k + 1)
            add_terms(k)
            for i, (lo, hi) in enumerate(PIECES):
                if lo // CHUNK == k:
                    weight(i)

        quantize_w3()
        for i in range(len(PIECES)):
            mix(i)
